import numpy as np
CORES = [24,26,29,31,48,50,53,55]
N = 8
TK = 256
NT = N * TK
EPS = 0.01
def setup_inputs(rng):
    x = (rng.standard_normal((N, 128, TK), dtype=np.float32) * (0.5 + np.arange(N, dtype=np.float32).reshape(N, 1, 1) / N) + rng.standard_normal((N, 128, 1), dtype=np.float32))
    return {"x": x}
def reference(x):
    X = x.astype(np.float64)
    mu = X.sum(axis=(0, 2)).reshape(1, 128, 1) / NT
    rs = 1.0 / np.sqrt(((X - mu) ** 2).sum(axis=(0, 2)).reshape(1, 128, 1) / NT + EPS)
    n = (X - mu) * rs
    return {"y": n.astype(np.float32)}

from concourse.bass import DstId, RemoteDMATransfer
from concourse.mybir import AluOpType, AxisListType, ActivationFunctionType

NR = 8
TK = 256
NT = NR * TK
EPS = 0.01
H = TK // 2
SLOT = 4
ENGINES = 8

SCRATCH = {
    "xb": ("sbuf", [128, TK], "float32"),
    "xs": ("sbuf", [128, TK], "float32"),
    "sq": ("sbuf", [128, TK], "float32"),
    "z": ("sbuf", [128, TK], "float32"),
    "yb": ("sbuf", [128, TK], "float32"),
    "land": ("sbuf", [128, NR * SLOT], "float32"),
    "qs": ("sbuf", [128, NR * 2], "float32"),
    "c": ("sbuf", [128, 8], "float32"),
}
SEMAPHORES = ["ld", "st", "pre", "loc", "rem", "snt", "tot", "v1", "v2", "v3", "sds", "fin", "out"]


def _lowest(mask, k):
    m, b = 0, 0
    while k:
        if (mask >> b) & 1:
            m |= 1 << b
            k -= 1
        b += 1
    return m


def _plan(cores, topo):
    forward = {c: [] for c in cores}
    for d in cores:
        for ch in sorted({topo.chip(c) for c in cores} - {topo.chip(d)}):
            able = [c for c in cores if topo.chip(c) == ch and topo.may_write(c, d)]
            near = [c for c in able if topo.die(c) == topo.die(d)] or able
            forward[min(near, key=lambda c: (len(forward[c]), c))].append(d)
    return forward


def rank_program(g, core, T, topo):
    rank = T.rank_of(core)
    if rank is None:
        return
    cores = list(T.cores)
    sem = T.sem
    forward = _plan(cores, topo)
    home = [c for c in cores if topo.chip(c) == topo.chip(core)]
    mates = sorted((c for c in home if c != core), key=lambda c: (not forward[c], c))
    blocks_in = sum(1 for c in cores if core in forward[c])

    allowed = -1
    for d in mates + forward[core]:
        allowed &= topo.mask(core, d)
    engines = _lowest(allowed, ENGINES)

    def ids(dsts):
        return [DstId(rid=topo.addr(d)[0], pnc=topo.addr(d)[1]) for d in dsts]

    o = rank * SLOT
    own = T.land[:, o:o + SLOT]
    b0 = T.rank_of(home[0]) * SLOT
    block = T.land[:, b0:b0 + len(home) * SLOT]
    n_loc = ENGINES * len(mates)
    n_rem = ENGINES * blocks_in
    S, nS, Ee, ve, iv, sd = (T.c[:, i:i + 1] for i in range(6))
    sums = T.land[:, 0:NR * SLOT:2]
    squares = T.land[:, 1:NR * SLOT:2]
    X, add, mult = AxisListType.X, AluOpType.add, AluOpType.mult
    A = ActivationFunctionType
    v, s, q = g.vector, g.scalar, g.sync

    q.dma_start(T.xb[:], T.x[:]).then_inc(sem.ld, 16)

    v.wait_ge(sem.ld, 16)
    s.wait_ge(sem.ld, 16)
    for h in range(2):
        cols = T.xb[:, h * H:(h + 1) * H]
        v.tensor_reduce(T.land[:, o + 2 * h:o + 2 * h + 1], cols, X, add).then_inc(sem.st, 1)
        s.activation(T.sq[:, h * H:(h + 1) * H], cols, A.Square,
                     accum_out=T.land[:, o + 2 * h + 1:o + 2 * h + 2]).then_inc(sem.st, 1)
    v.tensor_scalar(T.xs[:], T.xb[:], float(NT), None, mult).then_inc(sem.pre, 1)

    g.wait_ge(sem.st, 4)
    g.remote_dma_fused([RemoteDMATransfer(dst_ids=ids(mates), dma_engine_mask=engines, remote_sem=sem.loc,
                                          srcs=[own], dsts=[own] * len(mates))], local_sem=sem.snt)
    sent = ENGINES
    if forward[core]:
        g.wait_ge(sem.loc, n_loc)
        g.remote_dma_fused([RemoteDMATransfer(dst_ids=ids(forward[core]), dma_engine_mask=engines, remote_sem=sem.rem,
                                              srcs=[block], dsts=[block] * len(forward[core]))], local_sem=sem.snt)
        sent += ENGINES
    g.wait_ge(sem.snt, sent)

    for e in (v, s):
        e.wait_ge(sem.st, 4)
        e.wait_ge(sem.loc, n_loc)
        e.wait_ge(sem.rem, n_rem)
    v.tensor_reduce(S, sums, X, add).then_inc(sem.tot, 1)
    v.tensor_reduce(nS, sums, X, add, negate=True).then_inc(sem.tot, 1)
    s.activation(T.qs[:], squares, A.Identity, bias=EPS * NT * NT / (NR * 2), scale=float(NT),
                 accum_out=Ee).then_inc(sem.tot, 1)

    s.wait_ge(sem.tot, 3)
    s.activation(sd, S, A.Sqrt, bias=Ee, scale=nS).then_inc(sem.sds, 1)
    v.wait_ge(sem.tot, 3)
    v.tensor_scalar(ve, S, nS, Ee, mult, add).then_inc(sem.v1, 1)
    v.wait_ge(sem.v1, 1)
    v.reciprocal(iv, ve).then_inc(sem.v2, 1)
    v.wait_ge(sem.v2, 1)
    v.wait_ge(sem.pre, 1)
    v.tensor_scalar(T.z[:], T.xs[:], nS, iv, add, mult).then_inc(sem.v3, 1)

    for e in (v, s):
        e.wait_ge(sem.v3, 1)
        e.wait_ge(sem.sds, 1)
    v.tensor_scalar(T.yb[:, 0:H], T.z[:, 0:H], sd, None, mult).then_inc(sem.fin, 1)
    s.activation(T.yb[:, H:TK], T.z[:, H:TK], A.Copy, scale=sd).then_inc(sem.fin, 1)
    q.wait_ge(sem.fin, 2)
    q.dma_start(T.y[:], T.yb[:]).then_inc(sem.out, 16)
    q.wait_ge(sem.out, 16)
